import numpy as np, ml_dtypes
CORES = [10,14,66,70,74,78,82,86,90,94,106,110]
N = 12
F = 256
def setup_inputs(rng):
    return {"a": rng.standard_normal((N, 128, 128), dtype=np.float32).astype(ml_dtypes.bfloat16), "b": rng.standard_normal((N, 128, F), dtype=np.float32).astype(ml_dtypes.bfloat16)}
def setup_inputs_big(rng):
    d = setup_inputs(rng)
    for k in ("a", "b"): d[k] = (d[k].astype(np.float32) * 1024.0).astype(d[k].dtype)
    return d
def setup_inputs_small(rng):
    d = setup_inputs(rng)
    for k in ("a", "b"): d[k] = (d[k].astype(np.float32) * (1 / 1024.0)).astype(d[k].dtype)
    return d
def setup_inputs_apart(rng):
    d = setup_inputs(rng)
    f = (10.0 ** rng.permutation(np.linspace(-1.5, 1.5, N))).astype(np.float32).reshape(N, 1, 1)
    for k in ("a", "b"): d[k] = (d[k].astype(np.float32) * f).astype(d[k].dtype)
    return d
def reference(a, b):
    s = (a.astype(np.float64).sum(axis=0).T @ b.astype(np.float64).sum(axis=0)).astype(ml_dtypes.bfloat16 if a.dtype != np.float64 else np.float64)
    return {"y": np.broadcast_to(s, (N,) + s.shape)}

@@ -1,0 +1,128 @@
+from concourse.bass import DstId, RemoteDMATransfer
+
+NPIECE = 6
+WID = 64
+SCRATCH = {
+    "D": ("dram", [NPIECE, 128, WID], "bfloat16"),
+    "R": ("dram", [12, 128, WID], "bfloat16"),
+    "G": ("dram", [NPIECE, 128, WID], "bfloat16"),
+    "A": ("sbuf", [128, 128], "bfloat16"),
+    "B": ("sbuf", [128, 256], "bfloat16"),
+    "Y": ("sbuf", [128, 256], "bfloat16"),
+    "P": ("psum", [128, 256], "float32"),
+}
+SEMAPHORES = ["ld", "raw", "ga", "gb", "fin", "mm", "cp", "st", "loc"]
+FOLD_ENGINES = 8
+
+
+def _bits(mask):
+    return [e for e in range(mask.bit_length()) if (mask >> e) & 1]
+
+
+def _common(topo, src, dests):
+    m = topo.mask(src, dests[0])
+    for d in dests[1:]:
+        m &= topo.mask(src, d)
+    return m
+
+
+def _chips(T, topo):
+    chips = []
+    for c in T.cores:
+        if topo.chip(c) not in chips:
+            chips.append(topo.chip(c))
+    return chips
+
+
+def _fold_plan(T, topo, src):
+    dests = [c for c in T.cores if c != src and (topo.chip(c) == topo.chip(src) or topo.die(c) == topo.die(src))]
+    return dests, _bits(_common(topo, src, dests))[:FOLD_ENGINES]
+
+
+def _scatter_plan(T, topo, src):
+    chips = _chips(T, topo)
+    jobs = []
+    for k, ch in enumerate(chips):
+        dests = [c for c in T.cores if topo.chip(c) == ch and c != src]
+        jobs.append((k, dests))
+    jobs.sort(key=lambda j: (topo.chip(j[1][0]) == topo.chip(src), j[0]))
+    again = _fold_plan(T, topo, src)[1]
+    used, plan = [], []
+    for k, dests in jobs:
+        free = [e for e in _bits(_common(topo, src, dests)) if e not in used]
+        free.sort(key=lambda e: (e not in again, e % 2, e))
+        used.append(free[0])
+        plan.append((k, dests, [free[0]]))
+    return plan
+
+
+def _mask(engines):
+    m = 0
+    for e in engines:
+        m |= 1 << e
+    return m
+
+
+def _ids(topo, dests):
+    out = []
+    for d in dests:
+        rid, pid, _ = topo.addr(d)
+        out.append(DstId(rid=rid, pnc=pid))
+    return out
+
+
+def rank_program(g, core, T, topo):
+    rank = T.rank_of(core)
+    if rank is None:
+        return
+    S = T.sem
+    chips = _chips(T, topo)
+    mine = chips.index(topo.chip(core))
+    na = 2
+
+    raw_in = ga_in = gb_in = 0
+    for s in T.cores:
+        if s == core:
+            continue
+        for k, dests, eng in _scatter_plan(T, topo, s):
+            if core in dests:
+                raw_in += len(eng)
+        dests, eng = _fold_plan(T, topo, s)
+        if core in dests:
+            if chips.index(topo.chip(s)) < na:
+                ga_in += len(eng)
+            else:
+                gb_in += len(eng)
+
+    g.sync.dma_start(T.D[0:na], T.a[:, :]).then_inc(S.ld, 16)
+    g.scalar.dma_start(T.D[na:NPIECE], T.b[:, :]).then_inc(S.ld, 16)
+
+    g.wait_ge(S.ld, 32)
+    left = 0
+    trs = []
+    for k, dests, eng in _scatter_plan(T, topo, core):
+        trs.append(RemoteDMATransfer(dst_ids=_ids(topo, dests), dma_engine_mask=_mask(eng), remote_sem=S.raw,
+                                     srcs=[T.D[k]], dsts=[T.R[rank] for _ in dests], alu_op=0))
+        left += len(eng)
+    g.remote_dma_fused(trs, local_sem=S.loc)
+
+    g.wait_ge(S.raw, raw_in)
+    dests, eng = _fold_plan(T, topo, core)
+    srcs = [T.D[mine] if j == rank else T.R[j] for j in range(len(T.cores))]
+    g.remote_dma_fused([RemoteDMATransfer(dst_ids=_ids(topo, dests), dma_engine_mask=_mask(eng),
+                                          remote_sem=S.ga if mine < na else S.gb,
+                                          srcs=srcs, dsts=[T.G[mine] for _ in dests], alu_op=1)], local_sem=S.loc)
+    left += len(eng)
+
+    g.sync.wait_ge(S.ga, ga_in)
+    g.sync.dma_start(T.A[:, :], T.G[0:na]).then_inc(S.fin, 16)
+    g.scalar.wait_ge(S.gb, gb_in)
+    g.scalar.dma_start(T.B[:, :], T.G[na:NPIECE]).then_inc(S.fin, 16)
+    g.tensor.wait_ge(S.fin, 32)
+    g.tensor.matmul(T.P[:, :], T.A[:, :], T.B[:, :], True, True).then_inc(S.mm, 1)
+    g.vector.wait_ge(S.mm, 1)
+    g.vector.tensor_copy(T.Y[:, :], T.P[:, :]).then_inc(S.cp, 1)
+    g.sync.wait_ge(S.cp, 1)
+    g.sync.dma_start(T.y[:, :], T.Y[:, :]).then_inc(S.st, 16)
+    g.sync.wait_ge(S.st, 16)
+    g.wait_ge(S.loc, left)

@@ -1,59 +1,60 @@
 from concourse.bass import DstId, RemoteDMATransfer
 
-NPIECE = 6
-WID = 64
+NPIECE = 12
+NA = 4
+WID = 32
 SCRATCH = {
     "D": ("dram", [NPIECE, 128, WID], "bfloat16"),
-    "R": ("dram", [12, 128, WID], "bfloat16"),
+    "R": ("dram", [NPIECE, 128, WID], "bfloat16"),
     "G": ("dram", [NPIECE, 128, WID], "bfloat16"),
+    "I": ("dram", [129, 128], "bfloat16"),
+    "Z": ("sbuf", [128, 129], "bfloat16"),
+    "Sm": ("sbuf", [128, 128], "bfloat16"),
+    "Tr": ("sbuf", [128, 512], "bfloat16"),
+    "Own": ("sbuf", [128, 256], "bfloat16"),
     "A": ("sbuf", [128, 128], "bfloat16"),
     "B": ("sbuf", [128, 256], "bfloat16"),
     "Y": ("sbuf", [128, 256], "bfloat16"),
-    "P": ("psum", [128, 256], "float32"),
+    "P": ("psum", [128, 512], "float32"),
+    "P2": ("psum", [128, 512], "float32"),
 }
-SEMAPHORES = ["ld", "raw", "ga", "gb", "fin", "mm", "cp", "st", "loc"]
-FOLD_ENGINES = 8
+SEMAPHORES = ["ld", "own", "zs", "zm", "idn", "ss", "ts", "raw", "ga", "gb", "fin", "p2", "oc", "mm", "cp", "st", "loc"]
 
 
 def _bits(mask):
     return [e for e in range(mask.bit_length()) if (mask >> e) & 1]
 
 
-def _common(topo, src, dests):
-    m = topo.mask(src, dests[0])
-    for d in dests[1:]:
-        m &= topo.mask(src, d)
-    return m
-
-
-def _chips(T, topo):
-    chips = []
-    for c in T.cores:
-        if topo.chip(c) not in chips:
-            chips.append(topo.chip(c))
-    return chips
-
-
-def _fold_plan(T, topo, src):
-    dests = [c for c in T.cores if c != src and (topo.chip(c) == topo.chip(src) or topo.die(c) == topo.die(src))]
-    return dests, _bits(_common(topo, src, dests))[:FOLD_ENGINES]
+def _hops(topo, src, dst):
+    a, b = topo.chip(src), topo.chip(dst)
+    if a == b:
+        return 0
+    return 1 if (topo.mates(a, b) or topo.same_plane(a, b)) else 2
 
 
 def _scatter_plan(T, topo, src):
-    chips = _chips(T, topo)
-    jobs = []
-    for k, ch in enumerate(chips):
-        dests = [c for c in T.cores if topo.chip(c) == ch and c != src]
-        jobs.append((k, dests))
-    jobs.sort(key=lambda j: (topo.chip(j[1][0]) == topo.chip(src), j[0]))
-    again = _fold_plan(T, topo, src)[1]
-    used, plan = [], []
-    for k, dests in jobs:
-        free = [e for e in _bits(_common(topo, src, dests)) if e not in used]
-        free.sort(key=lambda e: (e not in again, e % 2, e))
-        used.append(free[0])
-        plan.append((k, dests, [free[0]]))
-    return plan
+    others = [(k, d) for k, d in enumerate(T.cores) if d != src]
+    off = [kd for kd in others if _hops(topo, src, kd[1]) > 0]
+    on = [kd for kd in others if _hops(topo, src, kd[1]) == 0]
+    off.sort(key=lambda kd: -_hops(topo, src, kd[1]))
+    eo = _bits(topo.mask(src, off[0][1]))
+    first = [(k, d, [eo[i]]) for i, (k, d) in enumerate(off[:len(eo)])]
+    second, at = [], 0
+    for k, d in off[len(eo):]:
+        second.append((k, d, eo[at:at + 2]))
+        at += 2
+    for k, d in on:
+        second.append((k, d, [e for e in eo[at:at + 4] if e in _bits(topo.mask(src, d))]))
+        at += 4
+    return [first, second]
+
+
+def _fold_plan(T, topo, src):
+    dests = [c for c in T.cores if c != src]
+    m = topo.mask(src, dests[0])
+    for d in dests[1:]:
+        m &= topo.mask(src, d)
+    return dests, _bits(m)
 
 
 def _mask(engines):
@@ -76,52 +77,103 @@ def rank_program(g, core, T, topo):
     if rank is None:
         return
     S = T.sem
-    chips = _chips(T, topo)
-    mine = chips.index(topo.chip(core))
-    na = 2
+    is_a = rank < NA
+    if is_a:
+        n, w, base, K, tiles = 32, 128, 32 * rank, 128, 3
+    else:
+        n, w, base, K, tiles = 16, 256, 16 * (rank - NA), 96, 2
+    spt = NPIECE // tiles
 
     raw_in = ga_in = gb_in = 0
-    for s in T.cores:
+    for j, s in enumerate(T.cores):
         if s == core:
             continue
-        for k, dests, eng in _scatter_plan(T, topo, s):
-            if core in dests:
-                raw_in += len(eng)
-        dests, eng = _fold_plan(T, topo, s)
-        if core in dests:
-            if chips.index(topo.chip(s)) < na:
-                ga_in += len(eng)
-            else:
-                gb_in += len(eng)
+        for call in _scatter_plan(T, topo, s):
+            for k, d, eng in call:
+                if d == core:
+                    raw_in += len(eng)
+        if j < NA:
+            ga_in += len(_fold_plan(T, topo, s)[1])
+        else:
+            gb_in += len(_fold_plan(T, topo, s)[1])
 
-    g.sync.dma_start(T.D[0:na], T.a[:, :]).then_inc(S.ld, 16)
-    g.scalar.dma_start(T.D[na:NPIECE], T.b[:, :]).then_inc(S.ld, 16)
+    g.vector.memset(T.Z[:, :], 0.0).then_inc(S.zs, 1)
+    g.vector.wait_ge(S.zs, 1)
+    g.vector.memset(T.Z[:, 0:1], 1.0).then_inc(S.zs, 1)
+    g.vector.memset(T.A[:, :] if is_a else T.B[:, :], 0.0).then_inc(S.zm, 1)
+
+    g.sync.dma_start(T.D[0:NA], T.a[:, :]).then_inc(S.ld, 16)
+    g.scalar.dma_start(T.D[NA:NPIECE], T.b[:, :]).then_inc(S.ld, 16)
+    src_own = T.a[base:base + n, :] if is_a else T.b[base:base + n, :]
+    g.sync.dma_start(T.R[rank], src_own).then_inc(S.own, 16)
+    g.scalar.wait_ge(S.zs, 2)
+    g.scalar.dma_start(T.I[:, :], T.Z[:, :]).then_inc(S.idn, 16)
+    g.scalar.wait_ge(S.idn, 16)
+    for r in range(K // n):
+        g.scalar.dma_start(T.Sm[r * n:(r + 1) * n, :], T.I[base:base + n, :]).then_inc(S.ss, 16)
 
     g.wait_ge(S.ld, 32)
     left = 0
-    trs = []
-    for k, dests, eng in _scatter_plan(T, topo, core):
-        trs.append(RemoteDMATransfer(dst_ids=_ids(topo, dests), dma_engine_mask=_mask(eng), remote_sem=S.raw,
-                                     srcs=[T.D[k]], dsts=[T.R[rank] for _ in dests], alu_op=0))
-        left += len(eng)
-    g.remote_dma_fused(trs, local_sem=S.loc)
+    for call in _scatter_plan(T, topo, core):
+        trs = []
+        for k, d, eng in call:
+            trs.append(RemoteDMATransfer(dst_ids=_ids(topo, [d]), dma_engine_mask=_mask(eng), remote_sem=S.raw,
+                                         srcs=[T.D[k]], dsts=[T.R[rank]], alu_op=0))
+            left += len(eng)
+        g.remote_dma_fused(trs, local_sem=S.loc)
 
     g.wait_ge(S.raw, raw_in)
     dests, eng = _fold_plan(T, topo, core)
-    srcs = [T.D[mine] if j == rank else T.R[j] for j in range(len(T.cores))]
+    srcs = [T.D[rank] if j == rank else T.R[j] for j in range(NPIECE)]
     g.remote_dma_fused([RemoteDMATransfer(dst_ids=_ids(topo, dests), dma_engine_mask=_mask(eng),
-                                          remote_sem=S.ga if mine < na else S.gb,
-                                          srcs=srcs, dsts=[T.G[mine] for _ in dests], alu_op=1)], local_sem=S.loc)
+                                          remote_sem=S.ga if is_a else S.gb,
+                                          srcs=srcs, dsts=[T.G[rank] for _ in dests], alu_op=1)], local_sem=S.loc)
     left += len(eng)
 
+    g.sync.wait_ge(S.own, 16)
+    g.sync.wait_ge(S.raw, raw_in)
+    for t in range(tiles):
+        g.sync.dma_start(T.Tr[0:K, t * w:(t + 1) * w], T.R[t * spt:(t + 1) * spt]).then_inc(S.ts, 16)
+    g.tensor.wait_ge(S.ss, 16 * (K // n))
+    g.tensor.wait_ge(S.ts, 16 * tiles)
+    for t in range(tiles):
+        mmi = g.tensor.matmul(T.P2[:, 0:w], T.Sm[0:K, :], T.Tr[0:K, t * w:(t + 1) * w], t == 0, t == tiles - 1)
+    mmi.then_inc(S.p2, 1)
+    g.vector.wait_ge(S.p2, 1)
+    g.vector.tensor_copy(T.Own[:, 0:w], T.P2[:, 0:w]).then_inc(S.oc, 1)
+
+    nfin = 0
     g.sync.wait_ge(S.ga, ga_in)
-    g.sync.dma_start(T.A[:, :], T.G[0:na]).then_inc(S.fin, 16)
     g.scalar.wait_ge(S.gb, gb_in)
-    g.scalar.dma_start(T.B[:, :], T.G[na:NPIECE]).then_inc(S.fin, 16)
-    g.tensor.wait_ge(S.fin, 32)
-    g.tensor.matmul(T.P[:, :], T.A[:, :], T.B[:, :], True, True).then_inc(S.mm, 1)
+    if is_a:
+        g.sync.wait_ge(S.zm, 1)
+        if rank > 0:
+            g.sync.dma_start(T.A[0:base, :], T.G[0:rank]).then_inc(S.fin, 16)
+            nfin += 16
+        if rank + 1 < NA:
+            g.sync.dma_start(T.A[base + n:128, :], T.G[rank + 1:NA]).then_inc(S.fin, 16)
+            nfin += 16
+        g.scalar.dma_start(T.B[:, :], T.G[NA:NPIECE]).then_inc(S.fin, 16)
+        nfin += 16
+    else:
+        g.sync.dma_start(T.A[:, :], T.G[0:NA]).then_inc(S.fin, 16)
+        nfin += 16
+        g.scalar.wait_ge(S.zm, 1)
+        if rank > NA:
+            g.scalar.dma_start(T.B[0:base, :], T.G[NA:rank]).then_inc(S.fin, 16)
+            nfin += 16
+        if rank + 1 < NPIECE:
+            g.scalar.dma_start(T.B[base + n:128, :], T.G[rank + 1:NPIECE]).then_inc(S.fin, 16)
+            nfin += 16
+    g.tensor.wait_ge(S.oc, 1)
+    g.tensor.wait_ge(S.fin, nfin)
+    g.tensor.matmul(T.P[:, 0:256], T.A[:, :], T.B[:, :], True, False)
+    if is_a:
+        g.tensor.matmul(T.P[:, 0:256], T.Own[:, 0:128], T.B[:, :], False, True).then_inc(S.mm, 1)
+    else:
+        g.tensor.matmul(T.P[:, 0:256], T.A[:, :], T.Own[:, 0:256], False, True).then_inc(S.mm, 1)
     g.vector.wait_ge(S.mm, 1)
-    g.vector.tensor_copy(T.Y[:, :], T.P[:, :]).then_inc(S.cp, 1)
+    g.vector.tensor_copy(T.Y[:, :], T.P[:, 0:256]).then_inc(S.cp, 1)
     g.sync.wait_ge(S.cp, 1)
     g.sync.dma_start(T.y[:, :], T.Y[:, :]).then_inc(S.st, 16)
     g.sync.wait_ge(S.st, 16)

@@ -9,6 +9,7 @@ SCRATCH = {
     "G": ("dram", [NPIECE, 128, WID], "bfloat16"),
     "I": ("dram", [129, 128], "bfloat16"),
     "Z": ("sbuf", [128, 129], "bfloat16"),
+    "Zr": ("sbuf", [128, WID], "bfloat16"),
     "Sm": ("sbuf", [128, 128], "bfloat16"),
     "Tr": ("sbuf", [128, 512], "bfloat16"),
     "Own": ("sbuf", [128, 256], "bfloat16"),
@@ -18,7 +19,7 @@ SCRATCH = {
     "P": ("psum", [128, 512], "float32"),
     "P2": ("psum", [128, 512], "float32"),
 }
-SEMAPHORES = ["ld", "own", "zs", "zm", "idn", "ss", "ts", "raw", "ga", "gb", "fin", "p2", "oc", "mm", "cp", "st", "loc"]
+SEMAPHORES = ["ld", "own", "zs", "zz", "idn", "ss", "ts", "raw", "ga", "gb", "fin", "p2", "oc", "mm", "cp", "st", "loc"]
 
 
 def _bits(mask):
@@ -78,6 +79,7 @@ def rank_program(g, core, T, topo):
         return
     S = T.sem
     is_a = rank < NA
+    partner = [c for c in T.cores if c != core and topo.chip(c) == topo.chip(core)][0]
     if is_a:
         n, w, base, K, tiles = 32, 128, 32 * rank, 128, 3
     else:
@@ -96,11 +98,16 @@ def rank_program(g, core, T, topo):
             ga_in += len(_fold_plan(T, topo, s)[1])
         else:
             gb_in += len(_fold_plan(T, topo, s)[1])
+    zin = len(_fold_plan(T, topo, partner)[1])
+    if is_a:
+        ga_in += zin
+    else:
+        gb_in += zin
 
+    g.vector.memset(T.Zr[:, :], 0.0).then_inc(S.zz, 1)
     g.vector.memset(T.Z[:, :], 0.0).then_inc(S.zs, 1)
     g.vector.wait_ge(S.zs, 1)
     g.vector.memset(T.Z[:, 0:1], 1.0).then_inc(S.zs, 1)
-    g.vector.memset(T.A[:, :] if is_a else T.B[:, :], 0.0).then_inc(S.zm, 1)
 
     g.sync.dma_start(T.D[0:NA], T.a[:, :]).then_inc(S.ld, 16)
     g.scalar.dma_start(T.D[NA:NPIECE], T.b[:, :]).then_inc(S.ld, 16)
@@ -112,18 +119,24 @@ def rank_program(g, core, T, topo):
     for r in range(K // n):
         g.scalar.dma_start(T.Sm[r * n:(r + 1) * n, :], T.I[base:base + n, :]).then_inc(S.ss, 16)
 
-    g.wait_ge(S.ld, 32)
     left = 0
+    dests, eng = _fold_plan(T, topo, core)
+    prank = T.rank_of(partner)
+    rid, pid, _ = topo.addr(partner)
+    g.wait_ge(S.zz, 1)
+    g.remote_dma(T.G[prank], T.Zr[:, :], S.ga if prank < NA else S.gb, S.loc, pid, rid, _mask(eng))
+    left += len(eng)
+
+    g.wait_ge(S.ld, 32)
     for call in _scatter_plan(T, topo, core):
         trs = []
-        for k, d, eng in call:
-            trs.append(RemoteDMATransfer(dst_ids=_ids(topo, [d]), dma_engine_mask=_mask(eng), remote_sem=S.raw,
+        for k, d, e1 in call:
+            trs.append(RemoteDMATransfer(dst_ids=_ids(topo, [d]), dma_engine_mask=_mask(e1), remote_sem=S.raw,
                                          srcs=[T.D[k]], dsts=[T.R[rank]], alu_op=0))
-            left += len(eng)
+            left += len(e1)
         g.remote_dma_fused(trs, local_sem=S.loc)
 
     g.wait_ge(S.raw, raw_in)
-    dests, eng = _fold_plan(T, topo, core)
     srcs = [T.D[rank] if j == rank else T.R[j] for j in range(NPIECE)]
     g.remote_dma_fused([RemoteDMATransfer(dst_ids=_ids(topo, dests), dma_engine_mask=_mask(eng),
                                           remote_sem=S.ga if is_a else S.gb,
@@ -142,31 +155,12 @@ def rank_program(g, core, T, topo):
     g.vector.wait_ge(S.p2, 1)
     g.vector.tensor_copy(T.Own[:, 0:w], T.P2[:, 0:w]).then_inc(S.oc, 1)
 
-    nfin = 0
     g.sync.wait_ge(S.ga, ga_in)
+    g.sync.dma_start(T.A[:, :], T.G[0:NA]).then_inc(S.fin, 16)
     g.scalar.wait_ge(S.gb, gb_in)
-    if is_a:
-        g.sync.wait_ge(S.zm, 1)
-        if rank > 0:
-            g.sync.dma_start(T.A[0:base, :], T.G[0:rank]).then_inc(S.fin, 16)
-            nfin += 16
-        if rank + 1 < NA:
-            g.sync.dma_start(T.A[base + n:128, :], T.G[rank + 1:NA]).then_inc(S.fin, 16)
-            nfin += 16
-        g.scalar.dma_start(T.B[:, :], T.G[NA:NPIECE]).then_inc(S.fin, 16)
-        nfin += 16
-    else:
-        g.sync.dma_start(T.A[:, :], T.G[0:NA]).then_inc(S.fin, 16)
-        nfin += 16
-        g.scalar.wait_ge(S.zm, 1)
-        if rank > NA:
-            g.scalar.dma_start(T.B[0:base, :], T.G[NA:rank]).then_inc(S.fin, 16)
-            nfin += 16
-        if rank + 1 < NPIECE:
-            g.scalar.dma_start(T.B[base + n:128, :], T.G[rank + 1:NPIECE]).then_inc(S.fin, 16)
-            nfin += 16
+    g.scalar.dma_start(T.B[:, :], T.G[NA:NPIECE]).then_inc(S.fin, 16)
     g.tensor.wait_ge(S.oc, 1)
-    g.tensor.wait_ge(S.fin, nfin)
+    g.tensor.wait_ge(S.fin, 32)
     g.tensor.matmul(T.P[:, 0:256], T.A[:, :], T.B[:, :], True, False)
     if is_a:
         g.tensor.matmul(T.P[:, 0:256], T.Own[:, 0:128], T.B[:, :], False, True).then_inc(S.mm, 1)

@@ -1,29 +1,45 @@
 from concourse.bass import DstId, RemoteDMATransfer
+from concourse.mybir import ActivationFunctionType, AluOpType
 
-NPIECE = 12
-NA = 4
-WID = 32
+NPIECE = 24
+NA = 8
+WID = 16
+NR = 12
+NB = 8
+KP = NR * NB
 SCRATCH = {
     "D": ("dram", [NPIECE, 128, WID], "bfloat16"),
-    "R": ("dram", [NPIECE, 128, WID], "bfloat16"),
+    "R": ("dram", [NR, 128, WID], "bfloat16"),
     "G": ("dram", [NPIECE, 128, WID], "bfloat16"),
-    "I": ("dram", [129, 128], "bfloat16"),
-    "Z": ("sbuf", [128, 129], "bfloat16"),
+    "W": ("sbuf", [128, KP], "bfloat16"),
+    "E": ("sbuf", [128, KP], "bfloat16"),
+    "S1": ("sbuf", [128, KP // 2], "bfloat16"),
+    "S2": ("sbuf", [128, KP // 4], "bfloat16"),
+    "S3": ("sbuf", [128, NB], "bfloat16"),
     "Zr": ("sbuf", [128, WID], "bfloat16"),
     "Sm": ("sbuf", [128, 128], "bfloat16"),
-    "Tr": ("sbuf", [128, 512], "bfloat16"),
+    "Tr": ("sbuf", [128, 256], "bfloat16"),
     "Own": ("sbuf", [128, 256], "bfloat16"),
     "A": ("sbuf", [128, 128], "bfloat16"),
     "B": ("sbuf", [128, 256], "bfloat16"),
     "Y": ("sbuf", [128, 256], "bfloat16"),
     "P": ("psum", [128, 512], "float32"),
     "P2": ("psum", [128, 512], "float32"),
+    "P3": ("psum", [128, 512], "float32"),
 }
-SEMAPHORES = ["ld", "own", "zs", "zz", "idn", "ss", "ts", "raw", "ga", "gb", "fin", "p2", "oc", "mm", "cp", "st", "loc"]
+SEMAPHORES = ["la", "lb", "own", "iw", "vs", "zz", "sr", "ts", "raw", "ga", "gb", "fa", "fb", "p2", "oc", "m0", "m1",
+              "cp", "st", "loc"]
 
 
 def _bits(mask):
     return [e for e in range(mask.bit_length()) if (mask >> e) & 1]
+
+
+def _mask(engines):
+    m = 0
+    for e in engines:
+        m |= 1 << e
+    return m
 
 
 def _hops(topo, src, dst):
@@ -33,36 +49,54 @@ def _hops(topo, src, dst):
     return 1 if (topo.mates(a, b) or topo.same_plane(a, b)) else 2
 
 
-def _scatter_plan(T, topo, src):
-    others = [(k, d) for k, d in enumerate(T.cores) if d != src]
-    off = [kd for kd in others if _hops(topo, src, kd[1]) > 0]
-    on = [kd for kd in others if _hops(topo, src, kd[1]) == 0]
-    off.sort(key=lambda kd: -_hops(topo, src, kd[1]))
-    eo = _bits(topo.mask(src, off[0][1]))
-    first = [(k, d, [eo[i]]) for i, (k, d) in enumerate(off[:len(eo)])]
-    second, at = [], 0
-    for k, d in off[len(eo):]:
-        second.append((k, d, eo[at:at + 2]))
-        at += 2
-    for k, d in on:
-        second.append((k, d, [e for e in eo[at:at + 4] if e in _bits(topo.mask(src, d))]))
-        at += 4
-    return [first, second]
+def _helper(T, topo, c):
+    for h in range(max(T.cores) + 8):
+        if h in T.cores or topo.chip(h) != topo.chip(c) or topo.die(h) != topo.die(c):
+            continue
+        if all(topo.may_write(h, d) for d in T.cores):
+            return h
+    return None
 
 
-def _fold_plan(T, topo, src):
+def _owners(T, topo):
+    hs = [_helper(T, topo, c) for c in T.cores]
+    return hs[:NA] + list(T.cores) + hs[NA:]
+
+
+def _seat(k):
+    if k < NA:
+        return k
+    return k - NA if k < NA + NR else k - NR
+
+
+def _off_engines(T, topo, src):
+    m = None
+    for d in T.cores:
+        if d != src:
+            m = topo.mask(src, d) if m is None else (m & topo.mask(src, d))
+    return _bits(m)
+
+
+def _scatter_plan(T, topo, owners, src):
+    others = [(k, d) for k, d in enumerate(owners) if d != src]
+    todo_a = [kd for kd in others if kd[0] < NA]
+    todo_b = [kd for kd in others if kd[0] >= NA]
+    todo_a.sort(key=lambda kd: -_hops(topo, src, kd[1]))
+    todo_b.sort(key=lambda kd: -_hops(topo, src, kd[1]))
+    eo = _off_engines(T, topo, src)
+    calls = [[(k, d, [eo[i]]) for i, (k, d) in enumerate(todo_a)]]
+    for at in range(0, len(todo_b), len(eo)):
+        calls.append([(k, d, [eo[i]]) for i, (k, d) in enumerate(todo_b[at:at + len(eo)])])
+    return calls
+
+
+def _fold_plan(T, topo, owners, src):
+    at = _seat(owners.index(src))
     dests = [c for c in T.cores if c != src]
-    m = topo.mask(src, dests[0])
-    for d in dests[1:]:
-        m &= topo.mask(src, d)
-    return dests, _bits(m)
-
-
-def _mask(engines):
-    m = 0
-    for e in engines:
-        m |= 1 << e
-    return m
+    dests.sort(key=lambda c: (-_hops(topo, src, c), (T.cores.index(c) - at) % len(T.cores)))
+    eo = _off_engines(T, topo, src)
+    h = len(eo) // 2
+    return [(dests[0::2], eo[:h]), (dests[1::2], eo[h:])]
 
 
 def _ids(topo, dests):
@@ -73,62 +107,102 @@ def _ids(topo, dests):
     return out
 
 
+def _fold(g, T, topo, owners, core, k, srcs):
+    S = T.sem
+    trs, left = [], 0
+    for dests, eng in _fold_plan(T, topo, owners, core):
+        trs.append(RemoteDMATransfer(dst_ids=_ids(topo, dests), dma_engine_mask=_mask(eng),
+                                     remote_sem=S.ga if k < NA else S.gb,
+                                     srcs=srcs, dsts=[T.G[k] for _ in dests], alu_op=1))
+        left += len(eng)
+    g.remote_dma_fused(trs, local_sem=S.loc)
+    return left
+
+
+def _helper_program(g, core, T, topo, owners, k):
+    S = T.sem
+    seat = _seat(k)
+    boss = T.cores[seat]
+    n, base = NB, NB * seat
+    eng = _off_engines(T, topo, core)
+    g.iota(T.W[:, :], [[-1, KP]], 0, 1, allow_small_or_imprecise_dtypes=True).then_inc(S.iw, 1)
+    g.vector.memset(T.Sm[:, :], 0.0).then_inc(S.vs, 1)
+    g.vector.wait_ge(S.iw, 1)
+    g.vector.tensor_scalar(T.E[:, :], T.W[:, :], 0.0, None, AluOpType.is_equal).then_inc(S.vs, 1)
+    cnt = 2
+    cur, width = T.E, KP
+    for nxt in (T.S1, T.S2):
+        h = width // 2
+        g.vector.wait_ge(S.vs, cnt)
+        g.vector.tensor_tensor(nxt[:, 0:h], cur[:, 0:h], cur[:, h:width], AluOpType.add).then_inc(S.vs, 1)
+        cnt += 1
+        cur, width = nxt, h
+    g.vector.wait_ge(S.vs, cnt)
+    g.vector.tensor_tensor(T.S3[:, 0:n], cur[:, 0:n], cur[:, n:2 * n], AluOpType.add).then_inc(S.vs, 1)
+    cnt += 1
+    g.vector.wait_ge(S.vs, cnt)
+    g.vector.tensor_tensor(T.Sm[:, base:base + n], T.S3[:, 0:n], cur[:, 2 * n:3 * n], AluOpType.add).then_inc(S.vs, 1)
+    cnt += 1
+    rid, pid, _ = topo.addr(boss)
+    g.wait_ge(S.vs, cnt)
+    g.remote_dma(T.Sm[:, :], T.Sm[:, :], S.sr, S.loc, pid, rid, _mask(eng))
+    left = len(eng)
+    g.wait_ge(S.raw, NR)
+    left += _fold(g, T, topo, owners, core, k, [T.R[j] for j in range(NR)])
+    g.wait_ge(S.loc, left)
+
+
 def rank_program(g, core, T, topo):
+    owners = _owners(T, topo)
+    if core not in owners:
+        return
+    kp = owners.index(core)
     rank = T.rank_of(core)
     if rank is None:
+        _helper_program(g, core, T, topo, owners, kp)
         return
     S = T.sem
-    is_a = rank < NA
     partner = [c for c in T.cores if c != core and topo.chip(c) == topo.chip(core)][0]
-    if is_a:
-        n, w, base, K, tiles = 32, 128, 32 * rank, 128, 3
-    else:
-        n, w, base, K, tiles = 16, 256, 16 * (rank - NA), 96, 2
-    spt = NPIECE // tiles
+    base = NB * rank
+    eng = _off_engines(T, topo, core)
 
     raw_in = ga_in = gb_in = 0
-    for j, s in enumerate(T.cores):
+    for s in T.cores:
         if s == core:
             continue
-        for call in _scatter_plan(T, topo, s):
-            for k, d, eng in call:
+        for call in _scatter_plan(T, topo, owners, s):
+            for k, d, e1 in call:
                 if d == core:
-                    raw_in += len(eng)
-        if j < NA:
-            ga_in += len(_fold_plan(T, topo, s)[1])
-        else:
-            gb_in += len(_fold_plan(T, topo, s)[1])
-    zin = len(_fold_plan(T, topo, partner)[1])
-    if is_a:
-        ga_in += zin
-    else:
-        gb_in += zin
+                    raw_in += len(e1)
+    for k, o in enumerate(owners):
+        if o == core:
+            continue
+        for dests, e1 in _fold_plan(T, topo, owners, o):
+            if core in dests:
+                if k < NA:
+                    ga_in += len(e1)
+                else:
+                    gb_in += len(e1)
+    gb_in += len(_off_engines(T, topo, partner))
+    sm_in = len(_off_engines(T, topo, _helper(T, topo, core)))
 
     g.vector.memset(T.Zr[:, :], 0.0).then_inc(S.zz, 1)
-    g.vector.memset(T.Z[:, :], 0.0).then_inc(S.zs, 1)
-    g.vector.wait_ge(S.zs, 1)
-    g.vector.memset(T.Z[:, 0:1], 1.0).then_inc(S.zs, 1)
 
-    g.sync.dma_start(T.D[0:NA], T.a[:, :]).then_inc(S.ld, 16)
-    g.scalar.dma_start(T.D[NA:NPIECE], T.b[:, :]).then_inc(S.ld, 16)
-    src_own = T.a[base:base + n, :] if is_a else T.b[base:base + n, :]
-    g.sync.dma_start(T.R[rank], src_own).then_inc(S.own, 16)
-    g.scalar.wait_ge(S.zs, 2)
-    g.scalar.dma_start(T.I[:, :], T.Z[:, :]).then_inc(S.idn, 16)
-    g.scalar.wait_ge(S.idn, 16)
-    for r in range(K // n):
-        g.scalar.dma_start(T.Sm[r * n:(r + 1) * n, :], T.I[base:base + n, :]).then_inc(S.ss, 16)
+    g.sync.dma_start(T.D[0:NA], T.a[:, :]).then_inc(S.la, 16)
+    g.scalar.dma_start(T.D[NA:NPIECE], T.b[:, :]).then_inc(S.lb, 16)
+    g.scalar.dma_start(T.R[rank], T.b[base:base + NB, :]).then_inc(S.own, 16)
 
     left = 0
-    dests, eng = _fold_plan(T, topo, core)
-    prank = T.rank_of(partner)
+    pk = owners.index(partner)
     rid, pid, _ = topo.addr(partner)
     g.wait_ge(S.zz, 1)
-    g.remote_dma(T.G[prank], T.Zr[:, :], S.ga if prank < NA else S.gb, S.loc, pid, rid, _mask(eng))
+    g.remote_dma(T.G[pk], T.Zr[:, :], S.gb, S.loc, pid, rid, _mask(eng))
     left += len(eng)
 
-    g.wait_ge(S.ld, 32)
-    for call in _scatter_plan(T, topo, core):
+    g.wait_ge(S.la, 16)
+    for c, call in enumerate(_scatter_plan(T, topo, owners, core)):
+        if c == 1:
+            g.wait_ge(S.lb, 16)
         trs = []
         for k, d, e1 in call:
             trs.append(RemoteDMATransfer(dst_ids=_ids(topo, [d]), dma_engine_mask=_mask(e1), remote_sem=S.raw,
@@ -137,38 +211,34 @@ def rank_program(g, core, T, topo):
         g.remote_dma_fused(trs, local_sem=S.loc)
 
     g.wait_ge(S.raw, raw_in)
-    srcs = [T.D[rank] if j == rank else T.R[j] for j in range(NPIECE)]
-    g.remote_dma_fused([RemoteDMATransfer(dst_ids=_ids(topo, dests), dma_engine_mask=_mask(eng),
-                                          remote_sem=S.ga if is_a else S.gb,
-                                          srcs=srcs, dsts=[T.G[rank] for _ in dests], alu_op=1)], local_sem=S.loc)
-    left += len(eng)
+    left += _fold(g, T, topo, owners, core, kp, [T.D[kp] if j == rank else T.R[j] for j in range(NR)])
 
-    g.sync.wait_ge(S.own, 16)
-    g.sync.wait_ge(S.raw, raw_in)
-    for t in range(tiles):
-        g.sync.dma_start(T.Tr[0:K, t * w:(t + 1) * w], T.R[t * spt:(t + 1) * spt]).then_inc(S.ts, 16)
-    g.tensor.wait_ge(S.ss, 16 * (K // n))
-    g.tensor.wait_ge(S.ts, 16 * tiles)
-    for t in range(tiles):
-        mmi = g.tensor.matmul(T.P2[:, 0:w], T.Sm[0:K, :], T.Tr[0:K, t * w:(t + 1) * w], t == 0, t == tiles - 1)
-    mmi.then_inc(S.p2, 1)
+    g.scalar.wait_ge(S.own, 16)
+    g.scalar.wait_ge(S.raw, raw_in)
+    g.scalar.dma_start(T.Tr[0:KP, :], T.R[0:NR]).then_inc(S.ts, 16)
+    g.tensor.wait_ge(S.sr, sm_in)
+    g.tensor.wait_ge(S.ts, 16)
+    g.tensor.matmul(T.P2[:, 0:256], T.Sm[0:KP, :], T.Tr[0:KP, :], True, True).then_inc(S.p2, 1)
     g.vector.wait_ge(S.p2, 1)
-    g.vector.tensor_copy(T.Own[:, 0:w], T.P2[:, 0:w]).then_inc(S.oc, 1)
+    g.vector.tensor_copy(T.Own[:, :], T.P2[:, 0:256]).then_inc(S.oc, 1)
 
     g.sync.wait_ge(S.ga, ga_in)
-    g.sync.dma_start(T.A[:, :], T.G[0:NA]).then_inc(S.fin, 16)
+    g.sync.dma_start(T.A[:, :], T.G[0:NA]).then_inc(S.fa, 16)
     g.scalar.wait_ge(S.gb, gb_in)
-    g.scalar.dma_start(T.B[:, :], T.G[NA:NPIECE]).then_inc(S.fin, 16)
+    g.scalar.dma_start(T.B[:, :], T.G[NA:NPIECE]).then_inc(S.fb, 16)
+    banks = [(T.P, 0, S.m0), (T.P3, 128, S.m1)]
     g.tensor.wait_ge(S.oc, 1)
-    g.tensor.wait_ge(S.fin, 32)
-    g.tensor.matmul(T.P[:, 0:256], T.A[:, :], T.B[:, :], True, False)
-    if is_a:
-        g.tensor.matmul(T.P[:, 0:256], T.Own[:, 0:128], T.B[:, :], False, True).then_inc(S.mm, 1)
-    else:
-        g.tensor.matmul(T.P[:, 0:256], T.A[:, :], T.Own[:, 0:256], False, True).then_inc(S.mm, 1)
-    g.vector.wait_ge(S.mm, 1)
-    g.vector.tensor_copy(T.Y[:, :], T.P[:, 0:256]).then_inc(S.cp, 1)
-    g.sync.wait_ge(S.cp, 1)
+    g.tensor.wait_ge(S.fa, 16)
+    for bank, c0, sm in banks:
+        g.tensor.matmul(bank[:, 0:128], T.A[:, :], T.Own[:, c0:c0 + 128], True, False)
+    g.tensor.wait_ge(S.fb, 16)
+    for bank, c0, sm in banks:
+        g.tensor.matmul(bank[:, 0:128], T.A[:, :], T.B[:, c0:c0 + 128], False, True).then_inc(sm, 1)
+    g.vector.wait_ge(S.m0, 1)
+    g.vector.tensor_copy(T.Y[:, 0:128], T.P[:, 0:128]).then_inc(S.cp, 1)
+    g.scalar.wait_ge(S.m1, 1)
+    g.scalar.activation(T.Y[:, 128:256], T.P3[:, 0:128], ActivationFunctionType.Copy).then_inc(S.cp, 1)
+    g.sync.wait_ge(S.cp, 2)
     g.sync.dma_start(T.y[:, :], T.Y[:, :]).then_inc(S.st, 16)
     g.sync.wait_ge(S.st, 16)
     g.wait_ge(S.loc, left)

from concourse.bass import DstId, RemoteDMATransfer
from concourse.mybir import ActivationFunctionType, AluOpType

NPIECE = 24
NA = 8
WID = 16
NR = 12
NB = 8
KP = NR * NB
SCRATCH = {
    "D": ("dram", [NPIECE, 128, WID], "bfloat16"),
    "R": ("dram", [NR, 128, WID], "bfloat16"),
    "G": ("dram", [NPIECE, 128, WID], "bfloat16"),
    "W": ("sbuf", [128, KP], "bfloat16"),
    "E": ("sbuf", [128, KP], "bfloat16"),
    "S1": ("sbuf", [128, KP // 2], "bfloat16"),
    "S2": ("sbuf", [128, KP // 4], "bfloat16"),
    "S3": ("sbuf", [128, NB], "bfloat16"),
    "Zr": ("sbuf", [128, WID], "bfloat16"),
    "Sm": ("sbuf", [128, 128], "bfloat16"),
    "Tr": ("sbuf", [128, 256], "bfloat16"),
    "Own": ("sbuf", [128, 256], "bfloat16"),
    "A": ("sbuf", [128, 128], "bfloat16"),
    "B": ("sbuf", [128, 256], "bfloat16"),
    "Y": ("sbuf", [128, 256], "bfloat16"),
    "P": ("psum", [128, 512], "float32"),
    "P2": ("psum", [128, 512], "float32"),
    "P3": ("psum", [128, 512], "float32"),
}
SEMAPHORES = ["la", "lb", "own", "iw", "vs", "zz", "sr", "ts", "raw", "ga", "gb", "fa", "fb", "p2", "oc", "m0", "m1",
              "cp", "st", "loc"]


def _bits(mask):
    return [e for e in range(mask.bit_length()) if (mask >> e) & 1]


def _mask(engines):
    m = 0
    for e in engines:
        m |= 1 << e
    return m


def _hops(topo, src, dst):
    a, b = topo.chip(src), topo.chip(dst)
    if a == b:
        return 0
    return 1 if (topo.mates(a, b) or topo.same_plane(a, b)) else 2


def _helper(T, topo, c):
    for h in range(max(T.cores) + 8):
        if h in T.cores or topo.chip(h) != topo.chip(c) or topo.die(h) != topo.die(c):
            continue
        if all(topo.may_write(h, d) for d in T.cores):
            return h
    return None


def _owners(T, topo):
    hs = [_helper(T, topo, c) for c in T.cores]
    return hs[:NA] + list(T.cores) + hs[NA:]


def _seat(k):
    if k < NA:
        return k
    return k - NA if k < NA + NR else k - NR


def _off_engines(T, topo, src):
    m = None
    for d in T.cores:
        if d != src:
            m = topo.mask(src, d) if m is None else (m & topo.mask(src, d))
    return _bits(m)


def _scatter_plan(T, topo, owners, src):
    others = [(k, d) for k, d in enumerate(owners) if d != src]
    todo_a = [kd for kd in others if kd[0] < NA]
    todo_b = [kd for kd in others if kd[0] >= NA]
    todo_a.sort(key=lambda kd: -_hops(topo, src, kd[1]))
    todo_b.sort(key=lambda kd: -_hops(topo, src, kd[1]))
    eo = _off_engines(T, topo, src)
    calls = [[(k, d, [eo[i]]) for i, (k, d) in enumerate(todo_a)]]
    for at in range(0, len(todo_b), len(eo)):
        calls.append([(k, d, [eo[i]]) for i, (k, d) in enumerate(todo_b[at:at + len(eo)])])
    return calls


def _fold_plan(T, topo, owners, src):
    at = _seat(owners.index(src))
    dests = [c for c in T.cores if c != src]
    dests.sort(key=lambda c: (-_hops(topo, src, c), (T.cores.index(c) - at) % len(T.cores)))
    eo = _off_engines(T, topo, src)
    h = len(eo) // 2
    return [(dests[0::2], eo[:h]), (dests[1::2], eo[h:])]


def _ids(topo, dests):
    out = []
    for d in dests:
        rid, pid, _ = topo.addr(d)
        out.append(DstId(rid=rid, pnc=pid))
    return out


def _fold(g, T, topo, owners, core, k, srcs):
    S = T.sem
    trs, left = [], 0
    for dests, eng in _fold_plan(T, topo, owners, core):
        trs.append(RemoteDMATransfer(dst_ids=_ids(topo, dests), dma_engine_mask=_mask(eng),
                                     remote_sem=S.ga if k < NA else S.gb,
                                     srcs=srcs, dsts=[T.G[k] for _ in dests], alu_op=1))
        left += len(eng)
    g.remote_dma_fused(trs, local_sem=S.loc)
    return left


def _helper_program(g, core, T, topo, owners, k):
    S = T.sem
    seat = _seat(k)
    boss = T.cores[seat]
    n, base = NB, NB * seat
    eng = _off_engines(T, topo, core)
    g.iota(T.W[:, :], [[-1, KP]], 0, 1, allow_small_or_imprecise_dtypes=True).then_inc(S.iw, 1)
    g.vector.memset(T.Sm[:, :], 0.0).then_inc(S.vs, 1)
    g.vector.wait_ge(S.iw, 1)
    g.vector.tensor_scalar(T.E[:, :], T.W[:, :], 0.0, None, AluOpType.is_equal).then_inc(S.vs, 1)
    cnt = 2
    cur, width = T.E, KP
    for nxt in (T.S1, T.S2):
        h = width // 2
        g.vector.wait_ge(S.vs, cnt)
        g.vector.tensor_tensor(nxt[:, 0:h], cur[:, 0:h], cur[:, h:width], AluOpType.add).then_inc(S.vs, 1)
        cnt += 1
        cur, width = nxt, h
    g.vector.wait_ge(S.vs, cnt)
    g.vector.tensor_tensor(T.S3[:, 0:n], cur[:, 0:n], cur[:, n:2 * n], AluOpType.add).then_inc(S.vs, 1)
    cnt += 1
    g.vector.wait_ge(S.vs, cnt)
    g.vector.tensor_tensor(T.Sm[:, base:base + n], T.S3[:, 0:n], cur[:, 2 * n:3 * n], AluOpType.add).then_inc(S.vs, 1)
    cnt += 1
    rid, pid, _ = topo.addr(boss)
    g.wait_ge(S.vs, cnt)
    g.remote_dma(T.Sm[:, :], T.Sm[:, :], S.sr, S.loc, pid, rid, _mask(eng))
    left = len(eng)
    g.wait_ge(S.raw, NR)
    left += _fold(g, T, topo, owners, core, k, [T.R[j] for j in range(NR)])
    g.wait_ge(S.loc, left)


def rank_program(g, core, T, topo):
    owners = _owners(T, topo)
    if core not in owners:
        return
    kp = owners.index(core)
    rank = T.rank_of(core)
    if rank is None:
        _helper_program(g, core, T, topo, owners, kp)
        return
    S = T.sem
    partner = [c for c in T.cores if c != core and topo.chip(c) == topo.chip(core)][0]
    base = NB * rank
    eng = _off_engines(T, topo, core)

    raw_in = ga_in = gb_in = 0
    for s in T.cores:
        if s == core:
            continue
        for call in _scatter_plan(T, topo, owners, s):
            for k, d, e1 in call:
                if d == core:
                    raw_in += len(e1)
    for k, o in enumerate(owners):
        if o == core:
            continue
        for dests, e1 in _fold_plan(T, topo, owners, o):
            if core in dests:
                if k < NA:
                    ga_in += len(e1)
                else:
                    gb_in += len(e1)
    gb_in += len(_off_engines(T, topo, partner))
    sm_in = len(_off_engines(T, topo, _helper(T, topo, core)))

    g.vector.memset(T.Zr[:, :], 0.0).then_inc(S.zz, 1)

    g.sync.dma_start(T.D[0:NA], T.a[:, :]).then_inc(S.la, 16)
    g.scalar.dma_start(T.D[NA:NPIECE], T.b[:, :]).then_inc(S.lb, 16)
    g.scalar.dma_start(T.R[rank], T.b[base:base + NB, :]).then_inc(S.own, 16)

    left = 0
    pk = owners.index(partner)
    rid, pid, _ = topo.addr(partner)
    g.wait_ge(S.zz, 1)
    g.remote_dma(T.G[pk], T.Zr[:, :], S.gb, S.loc, pid, rid, _mask(eng))
    left += len(eng)

    g.wait_ge(S.la, 16)
    for c, call in enumerate(_scatter_plan(T, topo, owners, core)):
        if c == 1:
            g.wait_ge(S.lb, 16)
        trs = []
        for k, d, e1 in call:
            trs.append(RemoteDMATransfer(dst_ids=_ids(topo, [d]), dma_engine_mask=_mask(e1), remote_sem=S.raw,
                                         srcs=[T.D[k]], dsts=[T.R[rank]], alu_op=0))
            left += len(e1)
        g.remote_dma_fused(trs, local_sem=S.loc)

    g.wait_ge(S.raw, raw_in)
    left += _fold(g, T, topo, owners, core, kp, [T.D[kp] if j == rank else T.R[j] for j in range(NR)])

    g.scalar.wait_ge(S.own, 16)
    g.scalar.wait_ge(S.raw, raw_in)
    g.scalar.dma_start(T.Tr[0:KP, :], T.R[0:NR]).then_inc(S.ts, 16)
    g.tensor.wait_ge(S.sr, sm_in)
    g.tensor.wait_ge(S.ts, 16)
    g.tensor.matmul(T.P2[:, 0:256], T.Sm[0:KP, :], T.Tr[0:KP, :], True, True).then_inc(S.p2, 1)
    g.vector.wait_ge(S.p2, 1)
    g.vector.tensor_copy(T.Own[:, :], T.P2[:, 0:256]).then_inc(S.oc, 1)

    g.sync.wait_ge(S.ga, ga_in)
    g.sync.dma_start(T.A[:, :], T.G[0:NA]).then_inc(S.fa, 16)
    g.scalar.wait_ge(S.gb, gb_in)
    g.scalar.dma_start(T.B[:, :], T.G[NA:NPIECE]).then_inc(S.fb, 16)
    banks = [(T.P, 0, S.m0), (T.P3, 128, S.m1)]
    g.tensor.wait_ge(S.oc, 1)
    g.tensor.wait_ge(S.fa, 16)
    for bank, c0, sm in banks:
        g.tensor.matmul(bank[:, 0:128], T.A[:, :], T.Own[:, c0:c0 + 128], True, False)
    g.tensor.wait_ge(S.fb, 16)
    for bank, c0, sm in banks:
        g.tensor.matmul(bank[:, 0:128], T.A[:, :], T.B[:, c0:c0 + 128], False, True).then_inc(sm, 1)
    g.vector.wait_ge(S.m0, 1)
    g.vector.tensor_copy(T.Y[:, 0:128], T.P[:, 0:128]).then_inc(S.cp, 1)
    g.scalar.wait_ge(S.m1, 1)
    g.scalar.activation(T.Y[:, 128:256], T.P3[:, 0:128], ActivationFunctionType.Copy).then_inc(S.cp, 1)
    g.sync.wait_ge(S.cp, 2)
    g.sync.dma_start(T.y[:, :], T.Y[:, :]).then_inc(S.st, 16)
    g.sync.wait_ge(S.st, 16)
    g.wait_ge(S.loc, left)
